import numpy as np
import ml_dtypes


def mxq(x, axis, fmt="e4m3"):
    dtype, down = {"e4m3": (ml_dtypes.float8_e4m3fn, 7), "e5m2": (ml_dtypes.float8_e5m2, 14)}[fmt]
    v = np.moveaxis(np.asarray(x, np.float32).astype(ml_dtypes.bfloat16).astype(np.float64), axis, -1)
    blocks = v.reshape(v.shape[:-1] + (-1, 32))
    amax = np.abs(blocks).max(-1, keepdims=True)
    byte = np.maximum(np.where(amax > 0, np.frexp(amax)[1] - 1 + 127, 0) - down, 1)
    scale = np.exp2(byte - 127.0)
    codes = (blocks / scale).astype(np.float32).astype(dtype).astype(np.float64)
    return np.moveaxis((codes * scale).reshape(v.shape), -1, axis)


WIDE = False


def mx_kscale(k):
    if not WIDE:
        return np.ones(k)
    levels = np.array([10, -10, 5, -5, 0])
    if k % 512:
        return np.exp2(np.random.permutation(np.resize(levels, k // 32))).repeat(32)
    a = np.empty((k // 512, 16))
    for p in range(k // 512):
        a[p, :8] = np.random.permutation(np.resize(levels, 8))
        for g in range(8):
            far = levels[np.abs(levels - a[p, g]) >= 10]
            a[p, g + 8] = far[np.random.randint(len(far))]
    return np.exp2(a.ravel()).repeat(32)


def f64(x):
    return np.asarray(x).astype(np.float64)


def striped(idx):
    return np.tile(idx.reshape(-1, 16).T, (8, 1)).astype(np.uint16)


def unstriped(offs):
    return offs[:16].T.reshape(-1).astype(np.int64)


def pack_weight(w):
    k, n = w.shape
    w = f64(np.asarray(w, np.float32).astype(ml_dtypes.bfloat16)).reshape(k // 32, 32, n)
    amax = np.abs(w).max(1)
    byte = np.clip(np.where(amax > 0, np.frexp(amax)[1] - 1 + 127 - 7, 1), 1, 254)
    scaled = (w * np.exp2(127.0 - byte)[:, None, :]).reshape(k, n).astype(np.float32)
    words = np.ascontiguousarray(scaled.reshape(k // 512, 128, 4, n).transpose(0, 1, 3, 2)).astype(ml_dtypes.float8_e4m3fn).view(np.uint8)
    return words, np.ascontiguousarray(byte.astype(np.uint8).reshape(k // 512, 16, n))


def unpack_weight(words, scales):
    g, p, n, _ = words.shape
    vals = np.ascontiguousarray(words).view(ml_dtypes.float8_e4m3fn).astype(np.float64) * np.repeat(np.exp2(scales.astype(np.float64) - 127.0), 8, axis=1)[..., None]
    return vals.transpose(0, 1, 3, 2).reshape(g * 512, n)


K, T, S, H, V, Z, W = 512, 2048, 512, 512, 256, 512, 2048
P = 2 ** 7


def setup_inputs():
    n = np.random.standard_normal
    s = mx_kscale(K)[:, None]
    packed_xT = pack_weight(n((K, T)) * s)
    packed_eT = pack_weight(n((K, W)) * s)
    return {
        "x_words": packed_xT[0],
        "x_scales": packed_xT[1],
        "w1": (n((K, H)) / np.sqrt(K) / s).astype(np.float32),
        "rel": (np.random.uniform(0.3, 1.2, (H, V))).astype(np.float32),
        "e_words": packed_eT[0],
        "e_scales": packed_eT[1],
        "unit": (np.random.uniform(0.6, 1.4, (K, 1)) / np.sqrt(K) / s).astype(np.float32),
        "off": (np.tile(np.random.uniform(0.0, 1.0, W), (P, 1))).astype(np.float32),
        "offs": striped(np.random.permutation(T)[:S]),
        "del_": striped(np.random.permutation(S)),
        "anc": striped(np.random.permutation(S)[:V]),
        "fpr": striped(np.random.permutation(W)[:Z]),
    }


def reference(x_words, x_scales, w1, rel, e_words, e_scales, unit, off, offs, del_, anc, fpr):
    xq = unpack_weight(x_words, x_scales)[:, unstriped(offs)]
    y = mxq(f64(w1), 0, "e4m3").T @ xq
    yd = y[:, unstriped(del_)]
    dif = y - yd
    bits = np.tanh(2.0 * dif)
    fp = bits[:, unstriped(anc)] * f64(rel)
    hid = f64(unit) * fp
    e_fpr = unpack_weight(e_words, e_scales)[:, unstriped(fpr)]
    sc = mxq(hid, 0, "e4m3").T @ e_fpr
    ks = np.exp(1.4 * np.tanh(sc))
    ko = ks * (f64(off)[:1][:, unstriped(fpr)])
    num = ko.sum(axis=1, keepdims=True)
    den = ks.sum(axis=1, keepdims=True)
    mo = num / den
    dt = f64(off)[:1][:, unstriped(fpr)] - mo
    return ks * dt

@@ -1,0 +1,212 @@
+from contextlib import ExitStack
+
+import concourse.mybir as mybir
+
+K, T, S, H, V, Z, W = 512, 2048, 512, 512, 256, 512, 2048
+FLOPS = 2 * K * H * S + 2 * H * V * Z
+
+F32 = mybir.dt.float32
+BF16 = mybir.dt.bfloat16
+I32 = mybir.dt.int32
+U32 = mybir.dt.uint32
+U16 = mybir.dt.uint16
+U8 = mybir.dt.uint8
+FP8X4 = mybir.dt.float8_e4m3fn_x4
+ACT = mybir.ActivationFunctionType
+ALU = mybir.AluOpType
+
+P = 128
+PACK = 4
+HALF = 256
+
+
+def tile_picked_yaudfpr_vote_p_kernel(
+    tc, x_words, x_scales, w1, rel, e_words, e_scales, unit, off, offs, del_, anc, fpr, out
+):
+    nc = tc.nc
+    with ExitStack() as ctx:
+        sb = ctx.enter_context(tc.tile_pool(name="sb", bufs=1))
+        ps = ctx.enter_context(tc.psum_pool(name="ps", bufs=1))
+
+        offs_t = sb.tile([P, S // 16], U16, name="offs_t")
+        del_t = sb.tile([P, S // 16], U16, name="del_t")
+        anc_t = sb.tile([P, V // 16], U16, name="anc_t")
+        fpr_t = sb.tile([P, Z // 16], U16, name="fpr_t")
+
+        x_tab = sb.tile([P, T], I32, name="x_tab")
+        e_tab = sb.tile([P, W], I32, name="e_tab")
+        xs_tab = sb.tile([P, T], U8, name="xs_tab")
+        es_tab = sb.tile([P, W], U8, name="es_tab")
+        w_raw = sb.tile([P, PACK, H], F32, name="w_raw", tag="w_raw")
+
+        def load_scales(tab, src, queue):
+            for q in range(4):
+                queue.dma_start(out=tab[32 * q : 32 * q + 4, :].bitcast(I32), in_=src[0, 4 * q : 4 * q + 4, :].bitcast(I32))
+
+        nc.gpsimd.memset(xs_tab[:].bitcast(I32), 0)
+        nc.vector.memset(es_tab[:].bitcast(I32), 0)
+        nc.sync.dma_start(offs_t[:], offs)
+        load_scales(xs_tab, x_scales, nc.scalar)
+        nc.sync.dma_start(out=w_raw[:], in_=w1.rearrange("(p j) c -> p j c", j=PACK))
+        nc.sync.dma_start(out=x_tab[:], in_=x_words[0].rearrange("p n t -> p (n t)").bitcast(I32))
+        nc.sync.dma_start(fpr_t[:], fpr)
+        load_scales(es_tab, e_scales, nc.sync)
+        nc.sync.dma_start(del_t[:], del_)
+        nc.sync.dma_start(anc_t[:], anc)
+        nc.sync.dma_start(out=e_tab[:], in_=e_words[0].rearrange("p n t -> p (n t)").bitcast(I32))
+
+        xs_pick = sb.tile([P, S], U8, name="xs_pick", align_bytes=64)
+        x_pick = [sb.tile([P, HALF], U32, name="x_pick%d" % c, align_bytes=64) for c in range(2)]
+        es_pick = sb.tile([P, Z], U8, name="es_pick", align_bytes=64)
+        e_pick = sb.tile([P, Z], U32, name="e_pick", align_bytes=64)
+        nc.vector.tensor_copy(xs_pick[:], xs_tab[:].indirect(offs_t[:]))
+
+        w_bf = [sb.tile([P, 2, P, PACK], BF16, name="w_bf%d" % u, tag="w_bf%d" % u, align_bytes=64) for u in range(2)]
+        w_cols = w_raw[:].rearrange("p j (m t) -> p m j t", t=PACK)
+        for u in range(2):
+            nc.scalar.copy(w_bf[u][:].rearrange("p t m j -> p m j t"), w_cols[:, :, :, 2 * u : 2 * u + 2])
+
+        w_codes = [sb.tile([P, P], U32, name="w_codes%d" % t, align_bytes=64) for t in range(PACK)]
+        w_scales = [sb.tile([P, P], U8, name="w_scales%d" % t, align_bytes=64) for t in range(PACK)]
+
+        def quantize_w(t):
+            nc.vector.quantize_mx(out=w_codes[t][:].bitcast(FP8X4), scales=w_scales[t][:], in_=w_bf[t // 2][:, t % 2].rearrange("p m j -> p (m j)"))
+
+        quantize_w(0)
+        quantize_w(1)
+        for c in range(2):
+            nc.vector.tensor_copy(x_pick[c][:], x_tab[:].bitcast(U32).indirect(offs_t[:, 16 * c : 16 * (c + 1)]))
+        quantize_w(2)
+        quantize_w(3)
+        nc.vector.tensor_copy(es_pick[:], es_tab[:].indirect(fpr_t[:]))
+
+        factors = sb.tile([P, PACK * V + PACK], F32, name="factors", tag="w_bf0", align_bytes=64)
+        off_tab = sb.tile([P, W], F32, name="off_tab", tag="w_raw")
+        nc.sync.dma_start(out=factors[:, : PACK * V], in_=rel.rearrange("(p t) v -> p (t v)", t=PACK))
+        nc.sync.dma_start(out=factors[:, PACK * V :], in_=unit.rearrange("(p t) o -> p (t o)", t=PACK))
+        nc.sync.dma_start(out=off_tab[:], in_=off)
+
+        y_ps = [[ps.tile([P, HALF], F32, name="y_ps%d%d" % (t, c), tag="bank%d%d" % (t, c)) for c in range(2)] for t in range(PACK)]
+        y_sb = [sb.tile([P, S], F32, name="y_sb%d" % t) for t in range(PACK)]
+        for t in range(PACK):
+            for c in range(2):
+                cols = slice(c * HALF, (c + 1) * HALF)
+                nc.tensor.matmul_mx(
+                    out=y_ps[t][c][:], lhsT=w_codes[t][:].bitcast(FP8X4), lhsT_scale=w_scales[t][:],
+                    rhs=x_pick[c][:].bitcast(FP8X4), rhs_scale=xs_pick[:, cols], start=True, stop=True,
+                )
+
+        def leave_bank(t, c, on_vector):
+            cols = slice(c * HALF, (c + 1) * HALF)
+            if on_vector:
+                nc.vector.tensor_copy(y_sb[t][:, cols], y_ps[t][c][:])
+            else:
+                nc.scalar.copy(y_sb[t][:, cols], y_ps[t][c][:])
+
+        yd = [[sb.tile([P, HALF], F32, name="yd%d%d" % (t, c)) for c in range(2)] for t in range(PACK)]
+        dif = [sb.tile([P, S], F32, name="dif%d" % t) for t in range(PACK)]
+        picked = [sb.tile([P, V], F32, name="picked%d" % t, tag="picked%d" % t) for t in range(PACK)]
+        bits = [sb.tile([P, V], F32, name="bits%d" % t) for t in range(PACK)]
+        hid = sb.tile([P, PACK, V], BF16, name="hid")
+
+        def gather(dst, window, on_vector):
+            if on_vector:
+                nc.vector.tensor_copy(dst, window)
+            else:
+                nc.scalar.activation(dst, window, ACT.Copy)
+
+        def fetch_delayed(t, c, on_vector):
+            gather(yd[t][c][:], y_sb[t][:].indirect(del_t[:, 16 * c : 16 * (c + 1)]), on_vector)
+
+        def subtract(t, c):
+            nc.vector.tensor_tensor(dif[t][:, c * HALF : (c + 1) * HALF], y_ps[t][c][:], yd[t][c][:], ALU.subtract)
+
+        def subtract_g(t, c):
+            cols = slice(c * HALF, (c + 1) * HALF)
+            nc.gpsimd.tensor_tensor(dif[t][:, cols], y_sb[t][:, cols], yd[t][c][:], ALU.subtract)
+
+        def anchors(t, on_vector):
+            gather(picked[t][:], dif[t][:].indirect(anc_t[:]), on_vector)
+
+        def squash(t):
+            nc.scalar.activation(bits[t][:], picked[t][:], ACT.Tanh, scale=2.0)
+
+        def weigh(t):
+            nc.vector.scalar_tensor_tensor(hid[:, t, :], bits[t][:], factors[:, PACK * V + t : PACK * V + t + 1], factors[:, t * V : (t + 1) * V], ALU.mult, ALU.mult)
+
+        def fetch_e():
+            nc.vector.tensor_copy(e_pick[:], e_tab[:].bitcast(U32).indirect(fpr_t[:]))
+
+        leave_bank(0, 0, False)
+        leave_bank(0, 1, False)
+        leave_bank(1, 0, False)
+        leave_bank(1, 1, False)
+        fetch_delayed(0, 0, True)
+        fetch_delayed(0, 1, True)
+        fetch_delayed(1, 0, False)
+        fetch_delayed(1, 1, False)
+        subtract(0, 0)
+        subtract(0, 1)
+        subtract(1, 0)
+        subtract(1, 1)
+        leave_bank(2, 0, False)
+        leave_bank(2, 1, False)
+        leave_bank(3, 0, False)
+        leave_bank(3, 1, False)
+        fetch_delayed(2, 0, True)
+        fetch_delayed(2, 1, True)
+        fetch_delayed(3, 0, False)
+        fetch_delayed(3, 1, False)
+        subtract(2, 0)
+        subtract(2, 1)
+        subtract(3, 0)
+        subtract(3, 1)
+        anchors(0, False)
+        squash(0)
+        anchors(1, False)
+        squash(1)
+        anchors(2, False)
+        squash(2)
+        anchors(3, False)
+        squash(3)
+        fetch_e()
+        weigh(0)
+        weigh(1)
+        weigh(2)
+        weigh(3)
+
+        off_pick = sb.tile([P, Z], F32, name="off_pick", tag="picked3")
+        nc.scalar.activation(off_pick[:], off_tab[:].indirect(fpr_t[:]), ACT.Copy)
+
+        sc_ps = [[ps.tile([P, HALF], F32, name="sc_ps%d%d" % (h, c), tag="bank%d%d" % (h, c)) for c in range(2)] for h in range(2)]
+        for h in range(2):
+            hid_il = sb.tile([P, P, PACK], BF16, name="hid_il%d" % h, align_bytes=64)
+            nc.vector.tensor_copy(
+                hid_il[:].rearrange("p (c i) t -> p c t i", i=4),
+                hid[:, :, h * P : (h + 1) * P].rearrange("p t (c i) -> p c t i", i=4),
+            )
+            h_codes = sb.tile([P, P], U32, name="h_codes%d" % h, align_bytes=64)
+            h_scales = sb.tile([P, P], U8, name="h_scales%d" % h, align_bytes=64)
+            nc.vector.quantize_mx(out=h_codes[:].bitcast(FP8X4), scales=h_scales[:], in_=hid_il[:].rearrange("p v t -> p (v t)"))
+            for c in range(2):
+                cols = slice(c * HALF, (c + 1) * HALF)
+                nc.tensor.matmul_mx(
+                    out=sc_ps[h][c][:], lhsT=h_codes[:].bitcast(FP8X4), lhsT_scale=h_scales[:],
+                    rhs=e_pick[:, cols].bitcast(FP8X4), rhs_scale=es_pick[:, cols], start=True, stop=True,
+                )
+
+        for h in range(2):
+            squashed = sb.tile([P, Z], F32, name="squashed%d" % h)
+            ks = sb.tile([P, Z], F32, name="ks%d" % h)
+            ko = sb.tile([P, Z], F32, name="ko%d" % h)
+            res = sb.tile([P, Z], F32, name="res%d" % h)
+            den = sb.tile([P, 1], F32, name="den%d" % h)
+            inv = sb.tile([P, 1], F32, name="inv%d" % h)
+            mo = sb.tile([P, 1], F32, name="mo%d" % h)
+            for c in range(2):
+                nc.scalar.activation(squashed[:, c * HALF : (c + 1) * HALF], sc_ps[h][c][:], ACT.Tanh)
+            nc.scalar.activation(ks[:], squashed[:], ACT.Exp, scale=1.4, accum_out=den[:])
+            nc.vector.reciprocal(inv[:], den[:])
+            nc.vector.scalar_tensor_tensor(ko[:], ks[:], inv[:], off_pick[:], ALU.mult, ALU.mult, accum_out=mo[:])
+            nc.vector.scalar_tensor_tensor(res[:], off_pick[:], mo[:], ks[:], ALU.subtract, ALU.mult)
+            nc.sync.dma_start(out=out[h * P : (h + 1) * P, :], in_=res[:])

@@ -26,6 +26,7 @@ def tile_picked_yaudfpr_vote_p_kernel(
     nc = tc.nc
     with ExitStack() as ctx:
         sb = ctx.enter_context(tc.tile_pool(name="sb", bufs=1))
+        stage = ctx.enter_context(tc.tile_pool(name="stage", bufs=1))
         ps = ctx.enter_context(tc.psum_pool(name="ps", bufs=1))
 
         offs_t = sb.tile([P, S // 16], U16, name="offs_t")
@@ -34,31 +35,28 @@ def tile_picked_yaudfpr_vote_p_kernel(
         fpr_t = sb.tile([P, Z // 16], U16, name="fpr_t")
 
         x_tab = sb.tile([P, T], I32, name="x_tab")
-        e_tab = sb.tile([P, W], I32, name="e_tab")
         xs_tab = sb.tile([P, T], U8, name="xs_tab")
         es_tab = sb.tile([P, W], U8, name="es_tab")
-        w_raw = sb.tile([P, PACK, H], F32, name="w_raw", tag="w_raw")
+        w_raw = stage.tile([P, PACK, H], F32, name="w_raw", offset=0)
 
         def load_scales(tab, src, queue):
             for q in range(4):
                 queue.dma_start(out=tab[32 * q : 32 * q + 4, :].bitcast(I32), in_=src[0, 4 * q : 4 * q + 4, :].bitcast(I32))
 
-        nc.gpsimd.memset(xs_tab[:].bitcast(I32), 0)
+        nc.gpsimd.memset(xs_tab[:, : T // 2].bitcast(I32), 0)
+        nc.vector.memset(xs_tab[:, T // 2 :].bitcast(I32), 0)
         nc.vector.memset(es_tab[:].bitcast(I32), 0)
         nc.sync.dma_start(offs_t[:], offs)
-        load_scales(xs_tab, x_scales, nc.scalar)
-        nc.sync.dma_start(out=w_raw[:], in_=w1.rearrange("(p j) c -> p j c", j=PACK))
-        nc.sync.dma_start(out=x_tab[:], in_=x_words[0].rearrange("p n t -> p (n t)").bitcast(I32))
         nc.sync.dma_start(fpr_t[:], fpr)
-        load_scales(es_tab, e_scales, nc.sync)
+        nc.sync.dma_start(out=w_raw[:], in_=w1.rearrange("(p j) c -> p j c", j=PACK))
+        load_scales(xs_tab, x_scales, nc.sync)
         nc.sync.dma_start(del_t[:], del_)
         nc.sync.dma_start(anc_t[:], anc)
-        nc.sync.dma_start(out=e_tab[:], in_=e_words[0].rearrange("p n t -> p (n t)").bitcast(I32))
+        nc.sync.dma_start(out=x_tab[:], in_=x_words[0].rearrange("p n t -> p (n t)").bitcast(I32))
+        load_scales(es_tab, e_scales, nc.sync)
 
         xs_pick = sb.tile([P, S], U8, name="xs_pick", align_bytes=64)
         x_pick = [sb.tile([P, HALF], U32, name="x_pick%d" % c, align_bytes=64) for c in range(2)]
-        es_pick = sb.tile([P, Z], U8, name="es_pick", align_bytes=64)
-        e_pick = sb.tile([P, Z], U32, name="e_pick", align_bytes=64)
         nc.vector.tensor_copy(xs_pick[:], xs_tab[:].indirect(offs_t[:]))
 
         w_bf = [sb.tile([P, 2, P, PACK], BF16, name="w_bf%d" % u, tag="w_bf%d" % u, align_bytes=64) for u in range(2)]
@@ -78,36 +76,37 @@ def tile_picked_yaudfpr_vote_p_kernel(
             nc.vector.tensor_copy(x_pick[c][:], x_tab[:].bitcast(U32).indirect(offs_t[:, 16 * c : 16 * (c + 1)]))
         quantize_w(2)
         quantize_w(3)
-        nc.vector.tensor_copy(es_pick[:], es_tab[:].indirect(fpr_t[:]))
 
-        factors = sb.tile([P, PACK * V + PACK], F32, name="factors", tag="w_bf0", align_bytes=64)
-        off_tab = sb.tile([P, W], F32, name="off_tab", tag="w_raw")
+        factors = stage.tile([P, PACK * V + PACK], F32, name="factors", offset=0)
+        e_tab = stage.tile([P, W], I32, name="e_tab", offset=4608)
+        off_tab = sb.tile([P, W], F32, name="off_tab", tag="w_bf1", align_bytes=64)
         nc.sync.dma_start(out=factors[:, : PACK * V], in_=rel.rearrange("(p t) v -> p (t v)", t=PACK))
         nc.sync.dma_start(out=factors[:, PACK * V :], in_=unit.rearrange("(p t) o -> p (t o)", t=PACK))
+        nc.sync.dma_start(out=e_tab[:], in_=e_words[0].rearrange("p n t -> p (n t)").bitcast(I32))
         nc.sync.dma_start(out=off_tab[:], in_=off)
 
-        y_ps = [[ps.tile([P, HALF], F32, name="y_ps%d%d" % (t, c), tag="bank%d%d" % (t, c)) for c in range(2)] for t in range(PACK)]
+        y_ps = []
+        for t in range(PACK):
+            if t < 2:
+                y_ps.append([ps.tile([P, HALF], F32, name="y_ps%d%d" % (t, c), tag="bank%d%d" % (t, c))[:] for c in range(2)])
+            else:
+                bank = ps.tile([P, S], F32, name="y_ps%d" % t)
+                y_ps.append([bank[:, :HALF], bank[:, HALF:], bank[:]])
         y_sb = [sb.tile([P, S], F32, name="y_sb%d" % t) for t in range(PACK)]
         for t in range(PACK):
             for c in range(2):
                 cols = slice(c * HALF, (c + 1) * HALF)
                 nc.tensor.matmul_mx(
-                    out=y_ps[t][c][:], lhsT=w_codes[t][:].bitcast(FP8X4), lhsT_scale=w_scales[t][:],
+                    out=y_ps[t][c], lhsT=w_codes[t][:].bitcast(FP8X4), lhsT_scale=w_scales[t][:],
                     rhs=x_pick[c][:].bitcast(FP8X4), rhs_scale=xs_pick[:, cols], start=True, stop=True,
                 )
 
-        def leave_bank(t, c, on_vector):
-            cols = slice(c * HALF, (c + 1) * HALF)
-            if on_vector:
-                nc.vector.tensor_copy(y_sb[t][:, cols], y_ps[t][c][:])
-            else:
-                nc.scalar.copy(y_sb[t][:, cols], y_ps[t][c][:])
-
-        yd = [[sb.tile([P, HALF], F32, name="yd%d%d" % (t, c)) for c in range(2)] for t in range(PACK)]
+        spans = [slice(0, HALF), slice(HALF, S), slice(0, S)]
+        yd = [stage.tile([P, S], F32, name="yd%d" % t, offset=12800 + 4096 * t) for t in range(PACK)]
         dif = [sb.tile([P, S], F32, name="dif%d" % t) for t in range(PACK)]
-        picked = [sb.tile([P, V], F32, name="picked%d" % t, tag="picked%d" % t) for t in range(PACK)]
-        bits = [sb.tile([P, V], F32, name="bits%d" % t) for t in range(PACK)]
-        hid = sb.tile([P, PACK, V], BF16, name="hid")
+        picked = sb.tile([P, 7, P], F32, name="picked")
+        bits = [sb.tile([P, P, PACK], F32, name="bits%d" % h) for h in range(2)]
+        weight = [stage.tile([P, P, PACK], F32, name="weight%d" % h, offset=12800 + 4096 - 1024 + 2048 * h) for h in range(2)]
 
         def gather(dst, window, on_vector):
             if on_vector:
@@ -115,98 +114,120 @@ def tile_picked_yaudfpr_vote_p_kernel(
             else:
                 nc.scalar.activation(dst, window, ACT.Copy)
 
+        def leave_bank(t, c, on_vector):
+            if on_vector:
+                nc.vector.tensor_copy(y_sb[t][:, spans[c]], y_ps[t][c])
+            else:
+                nc.scalar.copy(y_sb[t][:, spans[c]], y_ps[t][c])
+
         def fetch_delayed(t, c, on_vector):
-            gather(yd[t][c][:], y_sb[t][:].indirect(del_t[:, 16 * c : 16 * (c + 1)]), on_vector)
+            gather(yd[t][:, spans[c]], y_sb[t][:].indirect(del_t[:, 16 * c : 16 * (c + 1)]), on_vector)
 
         def subtract(t, c):
-            nc.vector.tensor_tensor(dif[t][:, c * HALF : (c + 1) * HALF], y_ps[t][c][:], yd[t][c][:], ALU.subtract)
+            nc.vector.tensor_tensor(dif[t][:, spans[c]], y_ps[t][c], yd[t][:, spans[c]], ALU.subtract)
 
         def subtract_g(t, c):
-            cols = slice(c * HALF, (c + 1) * HALF)
-            nc.gpsimd.tensor_tensor(dif[t][:, cols], y_sb[t][:, cols], yd[t][c][:], ALU.subtract)
+            nc.gpsimd.tensor_tensor(dif[t][:, spans[c]], y_sb[t][:, spans[c]], yd[t][:, spans[c]], ALU.subtract)
 
         def anchors(t, on_vector):
-            gather(picked[t][:], dif[t][:].indirect(anc_t[:]), on_vector)
+            dst = picked[:, 2 * t : 2 * t + 2, :].rearrange("p s v -> p (s v)")
+            gather(dst, dif[t][:].indirect(anc_t[:]), on_vector)
 
-        def squash(t):
-            nc.scalar.activation(bits[t][:], picked[t][:], ACT.Tanh, scale=2.0)
+        def anchors_half(t, h, on_vector):
+            gather(picked[:, 2 * t, :], dif[t][:].indirect(anc_t[:, 8 * h : 8 * (h + 1)]), on_vector)
 
-        def weigh(t):
-            nc.vector.scalar_tensor_tensor(hid[:, t, :], bits[t][:], factors[:, PACK * V + t : PACK * V + t + 1], factors[:, t * V : (t + 1) * V], ALU.mult, ALU.mult)
+        def squash(h):
+            if h == 0:
+                src = picked[:, 0::2, :].rearrange("p t v -> p v t")
+                dst = bits[h][:]
+            else:
+                src = picked[:, 1:7, :].rearrange("p (a s) v -> p v a s", s=3)[:, :, :, 0::2]
+                dst = bits[h][:].rearrange("p v (a b) -> p v a b", b=2)
+            nc.scalar.activation(dst, src, ACT.Tanh, scale=2.0)
+
+        def join_factors(h):
+            rel_h = factors[:, : PACK * V].rearrange("p (t v) -> p v t", t=PACK)[:, h * P : (h + 1) * P, :]
+            unit_b = factors[:, PACK * V :].unsqueeze(1).to_broadcast([P, P, PACK])
+            nc.gpsimd.tensor_tensor(weight[h][:], rel_h, unit_b, ALU.mult)
+
+        e_pick = stage.tile([P, Z], U32, name="e_pick", offset=12800 + 4096 * 3 + 1024, align_bytes=64)
 
         def fetch_e():
             nc.vector.tensor_copy(e_pick[:], e_tab[:].bitcast(U32).indirect(fpr_t[:]))
 
-        leave_bank(0, 0, False)
-        leave_bank(0, 1, False)
-        leave_bank(1, 0, False)
-        leave_bank(1, 1, False)
-        fetch_delayed(0, 0, True)
-        fetch_delayed(0, 1, True)
-        fetch_delayed(1, 0, False)
-        fetch_delayed(1, 1, False)
-        subtract(0, 0)
-        subtract(0, 1)
-        subtract(1, 0)
-        subtract(1, 1)
-        leave_bank(2, 0, False)
-        leave_bank(2, 1, False)
-        leave_bank(3, 0, False)
-        leave_bank(3, 1, False)
-        fetch_delayed(2, 0, True)
-        fetch_delayed(2, 1, True)
-        fetch_delayed(3, 0, False)
-        fetch_delayed(3, 1, False)
-        subtract(2, 0)
-        subtract(2, 1)
-        subtract(3, 0)
-        subtract(3, 1)
-        anchors(0, False)
-        squash(0)
-        anchors(1, False)
-        squash(1)
-        anchors(2, False)
-        squash(2)
-        anchors(3, False)
-        squash(3)
-        fetch_e()
-        weigh(0)
-        weigh(1)
-        weigh(2)
-        weigh(3)
+        es_pick = stage.tile([P, Z], U8, name="es_pick", offset=12800 + 4096 * 3, align_bytes=64)
 
-        off_pick = sb.tile([P, Z], F32, name="off_pick", tag="picked3")
-        nc.scalar.activation(off_pick[:], off_tab[:].indirect(fpr_t[:]), ACT.Copy)
+        def fetch_es():
+            nc.vector.tensor_copy(es_pick[:], es_tab[:].indirect(fpr_t[:]))
 
-        sc_ps = [[ps.tile([P, HALF], F32, name="sc_ps%d%d" % (h, c), tag="bank%d%d" % (h, c)) for c in range(2)] for h in range(2)]
-        for h in range(2):
-            hid_il = sb.tile([P, P, PACK], BF16, name="hid_il%d" % h, align_bytes=64)
-            nc.vector.tensor_copy(
-                hid_il[:].rearrange("p (c i) t -> p c t i", i=4),
-                hid[:, :, h * P : (h + 1) * P].rearrange("p t (c i) -> p c t i", i=4),
-            )
+        sc_ps = [[], []]
+
+        def score(h):
+            hid_il = stage.tile([P, P, PACK], BF16, name="hid%d" % h, offset=4608, align_bytes=64)
+            nc.vector.tensor_tensor(hid_il[:], bits[h][:], weight[h][:], ALU.mult)
             h_codes = sb.tile([P, P], U32, name="h_codes%d" % h, align_bytes=64)
             h_scales = sb.tile([P, P], U8, name="h_scales%d" % h, align_bytes=64)
             nc.vector.quantize_mx(out=h_codes[:].bitcast(FP8X4), scales=h_scales[:], in_=hid_il[:].rearrange("p v t -> p (v t)"))
             for c in range(2):
-                cols = slice(c * HALF, (c + 1) * HALF)
+                bank = ps.tile([P, HALF], F32, name="sc_ps%d%d" % (h, c), tag=("sc%d" % c if h == 0 else "bank0%d" % c))
+                sc_ps[h].append(bank)
                 nc.tensor.matmul_mx(
-                    out=sc_ps[h][c][:], lhsT=h_codes[:].bitcast(FP8X4), lhsT_scale=h_scales[:],
-                    rhs=e_pick[:, cols].bitcast(FP8X4), rhs_scale=es_pick[:, cols], start=True, stop=True,
+                    out=bank[:], lhsT=h_codes[:].bitcast(FP8X4), lhsT_scale=h_scales[:],
+                    rhs=e_pick[:, spans[c]].bitcast(FP8X4), rhs_scale=es_pick[:, spans[c]], start=True, stop=True,
                 )
+
+        leave_bank(0, 0, False)
+        leave_bank(1, 0, False)
+        leave_bank(0, 1, True)
+        leave_bank(1, 1, False)
+        fetch_delayed(0, 0, True)
+        fetch_delayed(0, 1, True)
+        leave_bank(2, 2, False)
+        leave_bank(3, 2, False)
+        fetch_delayed(1, 0, False)
+        fetch_delayed(1, 1, False)
+        subtract_g(0, 0)
+        subtract_g(0, 1)
+        fetch_delayed(2, 0, True)
+        fetch_delayed(2, 1, True)
+        fetch_delayed(3, 0, False)
+        fetch_delayed(3, 1, True)
+        subtract_g(1, 0)
+        subtract_g(1, 1)
+        join_factors(0)
+        join_factors(1)
+        subtract(2, 2)
+        subtract(3, 2)
+        fetch_es()
+        fetch_e()
+        anchors(0, False)
+        anchors(1, False)
+        anchors_half(2, 0, False)
+        anchors_half(3, 0, False)
+        squash(0)
+        score(0)
+        anchors_half(2, 1, False)
+        anchors_half(3, 1, False)
+        squash(1)
+        score(1)
+
+        off_pick = stage.tile([P, Z], F32, name="off_pick", offset=4608)
+        nc.vector.tensor_copy(off_pick[:], off_tab[:].indirect(fpr_t[:]))
 
         for h in range(2):
             squashed = sb.tile([P, Z], F32, name="squashed%d" % h)
             ks = sb.tile([P, Z], F32, name="ks%d" % h)
             ko = sb.tile([P, Z], F32, name="ko%d" % h)
-            res = sb.tile([P, Z], F32, name="res%d" % h)
             den = sb.tile([P, 1], F32, name="den%d" % h)
             inv = sb.tile([P, 1], F32, name="inv%d" % h)
             mo = sb.tile([P, 1], F32, name="mo%d" % h)
             for c in range(2):
-                nc.scalar.activation(squashed[:, c * HALF : (c + 1) * HALF], sc_ps[h][c][:], ACT.Tanh)
+                nc.scalar.activation(squashed[:, spans[c]], sc_ps[h][c][:], ACT.Tanh)
             nc.scalar.activation(ks[:], squashed[:], ACT.Exp, scale=1.4, accum_out=den[:])
             nc.vector.reciprocal(inv[:], den[:])
             nc.vector.scalar_tensor_tensor(ko[:], ks[:], inv[:], off_pick[:], ALU.mult, ALU.mult, accum_out=mo[:])
-            nc.vector.scalar_tensor_tensor(res[:], off_pick[:], mo[:], ks[:], ALU.subtract, ALU.mult)
-            nc.sync.dma_start(out=out[h * P : (h + 1) * P, :], in_=res[:])
+            for c in ([2] if h == 0 else [0, 1]):
+                res = sb.tile([P, Z], F32, name="res%d%d" % (h, c))
+                nc.vector.scalar_tensor_tensor(res[:, spans[c]], off_pick[:, spans[c]], mo[:], ks[:, spans[c]], ALU.subtract, ALU.mult)
+                queue = nc.scalar if c == 0 else nc.sync
+                queue.dma_start(out=out[h * P : (h + 1) * P, spans[c]], in_=res[:, spans[c]])

@@ -34,9 +34,9 @@ def tile_picked_yaudfpr_vote_p_kernel(
         anc_t = sb.tile([P, V // 16], U16, name="anc_t")
         fpr_t = sb.tile([P, Z // 16], U16, name="fpr_t")
 
-        x_tab = sb.tile([P, T], I32, name="x_tab")
+        x_tab = stage.tile([P, T], I32, name="x_tab", offset=29184)
         xs_tab = sb.tile([P, T], U8, name="xs_tab")
-        es_tab = sb.tile([P, W], U8, name="es_tab")
+        es_tab = stage.tile([P, W], U8, name="es_tab", offset=37376)
         w_raw = stage.tile([P, PACK, H], F32, name="w_raw", offset=0)
 
         def load_scales(tab, src, queue):
@@ -57,6 +57,7 @@ def tile_picked_yaudfpr_vote_p_kernel(
 
         xs_pick = sb.tile([P, S], U8, name="xs_pick", align_bytes=64)
         x_pick = [sb.tile([P, HALF], U32, name="x_pick%d" % c, align_bytes=64) for c in range(2)]
+        es_pick = sb.tile([P, Z], U8, name="es_pick", align_bytes=64)
         nc.vector.tensor_copy(xs_pick[:], xs_tab[:].indirect(offs_t[:]))
 
         w_bf = [sb.tile([P, 2, P, PACK], BF16, name="w_bf%d" % u, tag="w_bf%d" % u, align_bytes=64) for u in range(2)]
@@ -64,7 +65,8 @@ def tile_picked_yaudfpr_vote_p_kernel(
         for u in range(2):
             nc.scalar.copy(w_bf[u][:].rearrange("p t m j -> p m j t"), w_cols[:, :, :, 2 * u : 2 * u + 2])
 
-        w_codes = [sb.tile([P, P], U32, name="w_codes%d" % t, align_bytes=64) for t in range(PACK)]
+        w_codes = [sb.tile([P, P], U32, name="w_codes%d" % t, align_bytes=64) for t in range(2)]
+        w_codes.extend(stage.tile([P, P], U32, name="w_codes%d" % t, offset=29184 + 512 * t, align_bytes=64) for t in range(2, PACK))
         w_scales = [sb.tile([P, P], U8, name="w_scales%d" % t, align_bytes=64) for t in range(PACK)]
 
         def quantize_w(t):
@@ -90,7 +92,7 @@ def tile_picked_yaudfpr_vote_p_kernel(
             if t < 2:
                 y_ps.append([ps.tile([P, HALF], F32, name="y_ps%d%d" % (t, c), tag="bank%d%d" % (t, c))[:] for c in range(2)])
             else:
-                bank = ps.tile([P, S], F32, name="y_ps%d" % t)
+                bank = ps.tile([P, S], F32, name="y_ps%d" % t, tag="bank%d" % t)
                 y_ps.append([bank[:, :HALF], bank[:, HALF:], bank[:]])
         y_sb = [sb.tile([P, S], F32, name="y_sb%d" % t) for t in range(PACK)]
         for t in range(PACK):
@@ -103,7 +105,8 @@ def tile_picked_yaudfpr_vote_p_kernel(
 
         spans = [slice(0, HALF), slice(HALF, S), slice(0, S)]
         yd = [stage.tile([P, S], F32, name="yd%d" % t, offset=12800 + 4096 * t) for t in range(PACK)]
-        dif = [sb.tile([P, S], F32, name="dif%d" % t) for t in range(PACK)]
+        dif = [sb.tile([P, S], F32, name="dif%d" % t) for t in range(PACK - 1)]
+        dif.append(stage.tile([P, S], F32, name="dif3", offset=37376))
         picked = sb.tile([P, 7, P], F32, name="picked")
         bits = [sb.tile([P, P, PACK], F32, name="bits%d" % h) for h in range(2)]
         weight = [stage.tile([P, P, PACK], F32, name="weight%d" % h, offset=12800 + 4096 - 1024 + 2048 * h) for h in range(2)]
@@ -155,8 +158,6 @@ def tile_picked_yaudfpr_vote_p_kernel(
         def fetch_e():
             nc.vector.tensor_copy(e_pick[:], e_tab[:].bitcast(U32).indirect(fpr_t[:]))
 
-        es_pick = stage.tile([P, Z], U8, name="es_pick", offset=12800 + 4096 * 3, align_bytes=64)
-
         def fetch_es():
             nc.vector.tensor_copy(es_pick[:], es_tab[:].indirect(fpr_t[:]))
 
@@ -168,11 +169,14 @@ def tile_picked_yaudfpr_vote_p_kernel(
             h_codes = sb.tile([P, P], U32, name="h_codes%d" % h, align_bytes=64)
             h_scales = sb.tile([P, P], U8, name="h_scales%d" % h, align_bytes=64)
             nc.vector.quantize_mx(out=h_codes[:].bitcast(FP8X4), scales=h_scales[:], in_=hid_il[:].rearrange("p v t -> p (v t)"))
+            if h == 0:
+                sc_ps[h].extend(ps.tile([P, HALF], F32, name="sc_ps0%d" % c)[:] for c in range(2))
+            else:
+                bank = ps.tile([P, Z], F32, name="sc_ps1", tag="bank2")
+                sc_ps[h].extend([bank[:, spans[0]], bank[:, spans[1]], bank[:]])
             for c in range(2):
-                bank = ps.tile([P, HALF], F32, name="sc_ps%d%d" % (h, c), tag=("sc%d" % c if h == 0 else "bank0%d" % c))
-                sc_ps[h].append(bank)
                 nc.tensor.matmul_mx(
-                    out=bank[:], lhsT=h_codes[:].bitcast(FP8X4), lhsT_scale=h_scales[:],
+                    out=sc_ps[h][c], lhsT=h_codes[:].bitcast(FP8X4), lhsT_scale=h_scales[:],
                     rhs=e_pick[:, spans[c]].bitcast(FP8X4), rhs_scale=es_pick[:, spans[c]], start=True, stop=True,
                 )
 
@@ -191,14 +195,14 @@ def tile_picked_yaudfpr_vote_p_kernel(
         fetch_delayed(2, 0, True)
         fetch_delayed(2, 1, True)
         fetch_delayed(3, 0, False)
-        fetch_delayed(3, 1, True)
+        fetch_delayed(3, 1, False)
         subtract_g(1, 0)
         subtract_g(1, 1)
         join_factors(0)
         join_factors(1)
         subtract(2, 2)
-        subtract(3, 2)
         fetch_es()
+        subtract(3, 2)
         fetch_e()
         anchors(0, False)
         anchors(1, False)
@@ -221,8 +225,8 @@ def tile_picked_yaudfpr_vote_p_kernel(
             den = sb.tile([P, 1], F32, name="den%d" % h)
             inv = sb.tile([P, 1], F32, name="inv%d" % h)
             mo = sb.tile([P, 1], F32, name="mo%d" % h)
-            for c in range(2):
-                nc.scalar.activation(squashed[:, spans[c]], sc_ps[h][c][:], ACT.Tanh)
+            for c in ([0, 1] if h == 0 else [2]):
+                nc.scalar.activation(squashed[:, spans[c]], sc_ps[h][c], ACT.Tanh)
             nc.scalar.activation(ks[:], squashed[:], ACT.Exp, scale=1.4, accum_out=den[:])
             nc.vector.reciprocal(inv[:], den[:])
             nc.vector.scalar_tensor_tensor(ko[:], ks[:], inv[:], off_pick[:], ALU.mult, ALU.mult, accum_out=mo[:])

@@ -17,7 +17,20 @@ ALU = mybir.AluOpType
 
 P = 128
 PACK = 4
+PER_COLUMN = 16
 HALF = 256
+FIRST, SECOND, WHOLE = slice(0, HALF), slice(HALF, 2 * HALF), slice(0, 2 * HALF)
+HALVES = (FIRST, SECOND)
+SCALAR_SHARE = 384
+
+AT_W1 = 0
+AT_E_WORDS = 4608
+AT_YD = 12800
+YD_PITCH = 4096
+AT_WEIGHT = AT_YD + YD_PITCH - 1024
+AT_E_PICK = AT_YD + 3 * YD_PITCH + 1024
+AT_X_WORDS = 29184
+AT_E_SCALES = 37376
 
 
 def tile_picked_yaudfpr_vote_p_kernel(
@@ -26,22 +39,34 @@ def tile_picked_yaudfpr_vote_p_kernel(
     nc = tc.nc
     with ExitStack() as ctx:
         sb = ctx.enter_context(tc.tile_pool(name="sb", bufs=1))
-        stage = ctx.enter_context(tc.tile_pool(name="stage", bufs=1))
+        shared = ctx.enter_context(tc.tile_pool(name="shared", bufs=1))
         ps = ctx.enter_context(tc.psum_pool(name="ps", bufs=1))
 
-        offs_t = sb.tile([P, S // 16], U16, name="offs_t")
-        del_t = sb.tile([P, S // 16], U16, name="del_t")
-        anc_t = sb.tile([P, V // 16], U16, name="anc_t")
-        fpr_t = sb.tile([P, Z // 16], U16, name="fpr_t")
+        def entries(list_tile, span):
+            return list_tile[:, span.start // PER_COLUMN : span.stop // PER_COLUMN]
 
-        x_tab = stage.tile([P, T], I32, name="x_tab", offset=29184)
+        def on_vector(dst, src):
+            nc.vector.tensor_copy(dst, src)
+
+        def gather_on_scalar(dst, window):
+            nc.scalar.activation(dst, window, ACT.Copy)
+
+        offs_t = sb.tile([P, S // PER_COLUMN], U16, name="offs_t")
+        del_t = sb.tile([P, S // PER_COLUMN], U16, name="del_t")
+        anc_t = sb.tile([P, V // PER_COLUMN], U16, name="anc_t")
+        fpr_t = sb.tile([P, Z // PER_COLUMN], U16, name="fpr_t")
+        x_tab = shared.tile([P, T], I32, name="x_tab", offset=AT_X_WORDS)
         xs_tab = sb.tile([P, T], U8, name="xs_tab")
-        es_tab = stage.tile([P, W], U8, name="es_tab", offset=37376)
-        w_raw = stage.tile([P, PACK, H], F32, name="w_raw", offset=0)
+        es_tab = shared.tile([P, W], U8, name="es_tab", offset=AT_E_SCALES)
+        w_raw = shared.tile([P, PACK, H], F32, name="w_raw", offset=AT_W1)
 
-        def load_scales(tab, src, queue):
+        def load_words(tab, words):
+            nc.sync.dma_start(out=tab[:], in_=words[0].rearrange("p n j -> p (n j)").bitcast(I32))
+
+        def load_scales(tab, scales):
             for q in range(4):
-                queue.dma_start(out=tab[32 * q : 32 * q + 4, :].bitcast(I32), in_=src[0, 4 * q : 4 * q + 4, :].bitcast(I32))
+                rows = scales[0, 4 * q : 4 * q + 4, :]
+                nc.sync.dma_start(out=tab[32 * q : 32 * q + 4, :].bitcast(I32), in_=rows.bitcast(I32))
 
         nc.gpsimd.memset(xs_tab[:, : T // 2].bitcast(I32), 0)
         nc.vector.memset(xs_tab[:, T // 2 :].bitcast(I32), 0)
@@ -49,189 +74,178 @@ def tile_picked_yaudfpr_vote_p_kernel(
         nc.sync.dma_start(offs_t[:], offs)
         nc.sync.dma_start(fpr_t[:], fpr)
         nc.sync.dma_start(out=w_raw[:], in_=w1.rearrange("(p j) c -> p j c", j=PACK))
-        load_scales(xs_tab, x_scales, nc.sync)
+        load_scales(xs_tab, x_scales)
         nc.sync.dma_start(del_t[:], del_)
         nc.sync.dma_start(anc_t[:], anc)
-        nc.sync.dma_start(out=x_tab[:], in_=x_words[0].rearrange("p n t -> p (n t)").bitcast(I32))
-        load_scales(es_tab, e_scales, nc.sync)
+        load_words(x_tab, x_words)
+        load_scales(es_tab, e_scales)
 
         xs_pick = sb.tile([P, S], U8, name="xs_pick", align_bytes=64)
         x_pick = [sb.tile([P, HALF], U32, name="x_pick%d" % c, align_bytes=64) for c in range(2)]
         es_pick = sb.tile([P, Z], U8, name="es_pick", align_bytes=64)
-        nc.vector.tensor_copy(xs_pick[:], xs_tab[:].indirect(offs_t[:]))
+        on_vector(xs_pick[:], xs_tab[:].indirect(offs_t[:]))
 
         w_bf = [sb.tile([P, 2, P, PACK], BF16, name="w_bf%d" % u, tag="w_bf%d" % u, align_bytes=64) for u in range(2)]
         w_cols = w_raw[:].rearrange("p j (m t) -> p m j t", t=PACK)
         for u in range(2):
-            nc.scalar.copy(w_bf[u][:].rearrange("p t m j -> p m j t"), w_cols[:, :, :, 2 * u : 2 * u + 2])
+            nc.scalar.copy(w_bf[u][:].rearrange("p s m j -> p m j s"), w_cols[:, :, :, 2 * u : 2 * u + 2])
 
         w_codes = [sb.tile([P, P], U32, name="w_codes%d" % t, align_bytes=64) for t in range(2)]
-        w_codes.extend(stage.tile([P, P], U32, name="w_codes%d" % t, offset=29184 + 512 * t, align_bytes=64) for t in range(2, PACK))
+        for t in range(2, PACK):
+            w_codes.append(shared.tile([P, P], U32, name="w_codes%d" % t, offset=AT_X_WORDS + 4 * P * t, align_bytes=64))
         w_scales = [sb.tile([P, P], U8, name="w_scales%d" % t, align_bytes=64) for t in range(PACK)]
 
         def quantize_w(t):
-            nc.vector.quantize_mx(out=w_codes[t][:].bitcast(FP8X4), scales=w_scales[t][:], in_=w_bf[t // 2][:, t % 2].rearrange("p m j -> p (m j)"))
+            values = w_bf[t // 2][:, t % 2].rearrange("p m j -> p (m j)")
+            nc.vector.quantize_mx(out=w_codes[t][:].bitcast(FP8X4), scales=w_scales[t][:], in_=values)
 
         quantize_w(0)
         quantize_w(1)
         for c in range(2):
-            nc.vector.tensor_copy(x_pick[c][:], x_tab[:].bitcast(U32).indirect(offs_t[:, 16 * c : 16 * (c + 1)]))
+            on_vector(x_pick[c][:], x_tab[:].bitcast(U32).indirect(entries(offs_t, HALVES[c])))
         quantize_w(2)
         quantize_w(3)
 
-        factors = stage.tile([P, PACK * V + PACK], F32, name="factors", offset=0)
-        e_tab = stage.tile([P, W], I32, name="e_tab", offset=4608)
+        factors = shared.tile([P, PACK * V + PACK], F32, name="factors", offset=AT_W1)
+        e_tab = shared.tile([P, W], I32, name="e_tab", offset=AT_E_WORDS)
         off_tab = sb.tile([P, W], F32, name="off_tab", tag="w_bf1", align_bytes=64)
         nc.sync.dma_start(out=factors[:, : PACK * V], in_=rel.rearrange("(p t) v -> p (t v)", t=PACK))
         nc.sync.dma_start(out=factors[:, PACK * V :], in_=unit.rearrange("(p t) o -> p (t o)", t=PACK))
-        nc.sync.dma_start(out=e_tab[:], in_=e_words[0].rearrange("p n t -> p (n t)").bitcast(I32))
+        load_words(e_tab, e_words)
         nc.sync.dma_start(out=off_tab[:], in_=off)
 
-        y_ps = []
-        for t in range(PACK):
-            if t < 2:
-                y_ps.append([ps.tile([P, HALF], F32, name="y_ps%d%d" % (t, c), tag="bank%d%d" % (t, c))[:] for c in range(2)])
-            else:
-                bank = ps.tile([P, S], F32, name="y_ps%d" % t, tag="bank%d" % t)
-                y_ps.append([bank[:, :HALF], bank[:, HALF:], bank[:]])
+        y_ps = {}
+        for t in range(2):
+            for c in range(2):
+                y_ps[t, HALVES[c].start] = ps.tile([P, HALF], F32, name="y_ps%d%d" % (t, c))
+        y_bank = {t: ps.tile([P, S], F32, name="y_bank%d" % t, tag="y_bank%d" % t) for t in range(2, PACK)}
+
+        def y_in_psum(t, span):
+            return y_ps[t, span.start][:] if t < 2 else y_bank[t][:, span]
+
         y_sb = [sb.tile([P, S], F32, name="y_sb%d" % t) for t in range(PACK)]
         for t in range(PACK):
             for c in range(2):
-                cols = slice(c * HALF, (c + 1) * HALF)
                 nc.tensor.matmul_mx(
-                    out=y_ps[t][c], lhsT=w_codes[t][:].bitcast(FP8X4), lhsT_scale=w_scales[t][:],
-                    rhs=x_pick[c][:].bitcast(FP8X4), rhs_scale=xs_pick[:, cols], start=True, stop=True,
+                    out=y_in_psum(t, HALVES[c]), lhsT=w_codes[t][:].bitcast(FP8X4), lhsT_scale=w_scales[t][:],
+                    rhs=x_pick[c][:].bitcast(FP8X4), rhs_scale=xs_pick[:, HALVES[c]], start=True, stop=True,
                 )
 
-        spans = [slice(0, HALF), slice(HALF, S), slice(0, S)]
-        yd = [stage.tile([P, S], F32, name="yd%d" % t, offset=12800 + 4096 * t) for t in range(PACK)]
+        yd = [shared.tile([P, S], F32, name="yd%d" % t, offset=AT_YD + YD_PITCH * t) for t in range(PACK)]
         dif = [sb.tile([P, S], F32, name="dif%d" % t) for t in range(PACK - 1)]
-        dif.append(stage.tile([P, S], F32, name="dif3", offset=37376))
+        dif.append(shared.tile([P, S], F32, name="dif3", offset=AT_E_SCALES))
         picked = sb.tile([P, 7, P], F32, name="picked")
         bits = [sb.tile([P, P, PACK], F32, name="bits%d" % h) for h in range(2)]
-        weight = [stage.tile([P, P, PACK], F32, name="weight%d" % h, offset=12800 + 4096 - 1024 + 2048 * h) for h in range(2)]
+        weight = [shared.tile([P, P, PACK], F32, name="weight%d" % h, offset=AT_WEIGHT + 4 * P * PACK * h) for h in range(2)]
+        e_pick = shared.tile([P, Z], U32, name="e_pick", offset=AT_E_PICK, align_bytes=64)
 
-        def gather(dst, window, on_vector):
-            if on_vector:
-                nc.vector.tensor_copy(dst, window)
-            else:
-                nc.scalar.activation(dst, window, ACT.Copy)
+        def leave_psum(t, span, copy):
+            copy(y_sb[t][:, span], y_in_psum(t, span))
 
-        def leave_bank(t, c, on_vector):
-            if on_vector:
-                nc.vector.tensor_copy(y_sb[t][:, spans[c]], y_ps[t][c])
-            else:
-                nc.scalar.copy(y_sb[t][:, spans[c]], y_ps[t][c])
+        def fetch_delayed(t, span, gather):
+            gather(yd[t][:, span], y_sb[t][:].indirect(entries(del_t, span)))
 
-        def fetch_delayed(t, c, on_vector):
-            gather(yd[t][:, spans[c]], y_sb[t][:].indirect(del_t[:, 16 * c : 16 * (c + 1)]), on_vector)
+        def subtract_on_gpsimd(t):
+            for span in HALVES:
+                nc.gpsimd.tensor_tensor(dif[t][:, span], y_sb[t][:, span], yd[t][:, span], ALU.subtract)
 
-        def subtract(t, c):
-            nc.vector.tensor_tensor(dif[t][:, spans[c]], y_ps[t][c], yd[t][:, spans[c]], ALU.subtract)
+        def subtract_on_vector(t):
+            nc.vector.tensor_tensor(dif[t][:], y_in_psum(t, WHOLE), yd[t][:], ALU.subtract)
 
-        def subtract_g(t, c):
-            nc.gpsimd.tensor_tensor(dif[t][:, spans[c]], y_sb[t][:, spans[c]], yd[t][:, spans[c]], ALU.subtract)
+        def fetch_anchors(t):
+            gather_on_scalar(picked[:, 2 * t : 2 * t + 2, :].rearrange("p h v -> p (h v)"), dif[t][:].indirect(anc_t[:]))
 
-        def anchors(t, on_vector):
-            dst = picked[:, 2 * t : 2 * t + 2, :].rearrange("p s v -> p (s v)")
-            gather(dst, dif[t][:].indirect(anc_t[:]), on_vector)
-
-        def anchors_half(t, h, on_vector):
-            gather(picked[:, 2 * t, :], dif[t][:].indirect(anc_t[:, 8 * h : 8 * (h + 1)]), on_vector)
-
-        def squash(h):
-            if h == 0:
-                src = picked[:, 0::2, :].rearrange("p t v -> p v t")
-                dst = bits[h][:]
-            else:
-                src = picked[:, 1:7, :].rearrange("p (a s) v -> p v a s", s=3)[:, :, :, 0::2]
-                dst = bits[h][:].rearrange("p v (a b) -> p v a b", b=2)
-            nc.scalar.activation(dst, src, ACT.Tanh, scale=2.0)
+        def fetch_anchor_half(t, h):
+            gather_on_scalar(picked[:, 2 * t, :], dif[t][:].indirect(entries(anc_t, slice(h * P, (h + 1) * P))))
 
         def join_factors(h):
             rel_h = factors[:, : PACK * V].rearrange("p (t v) -> p v t", t=PACK)[:, h * P : (h + 1) * P, :]
             unit_b = factors[:, PACK * V :].unsqueeze(1).to_broadcast([P, P, PACK])
             nc.gpsimd.tensor_tensor(weight[h][:], rel_h, unit_b, ALU.mult)
 
-        e_pick = stage.tile([P, Z], U32, name="e_pick", offset=12800 + 4096 * 3 + 1024, align_bytes=64)
-
-        def fetch_e():
-            nc.vector.tensor_copy(e_pick[:], e_tab[:].bitcast(U32).indirect(fpr_t[:]))
-
-        def fetch_es():
-            nc.vector.tensor_copy(es_pick[:], es_tab[:].indirect(fpr_t[:]))
-
-        sc_ps = [[], []]
-
-        def score(h):
-            hid_il = stage.tile([P, P, PACK], BF16, name="hid%d" % h, offset=4608, align_bytes=64)
-            nc.vector.tensor_tensor(hid_il[:], bits[h][:], weight[h][:], ALU.mult)
+        def score(h, hid, banks):
+            nc.vector.tensor_tensor(hid, bits[h][:].rearrange("p v t -> p (v t)"), weight[h][:].rearrange("p v t -> p (v t)"), ALU.mult)
             h_codes = sb.tile([P, P], U32, name="h_codes%d" % h, align_bytes=64)
             h_scales = sb.tile([P, P], U8, name="h_scales%d" % h, align_bytes=64)
-            nc.vector.quantize_mx(out=h_codes[:].bitcast(FP8X4), scales=h_scales[:], in_=hid_il[:].rearrange("p v t -> p (v t)"))
-            if h == 0:
-                sc_ps[h].extend(ps.tile([P, HALF], F32, name="sc_ps0%d" % c)[:] for c in range(2))
-            else:
-                bank = ps.tile([P, Z], F32, name="sc_ps1", tag="bank2")
-                sc_ps[h].extend([bank[:, spans[0]], bank[:, spans[1]], bank[:]])
+            nc.vector.quantize_mx(out=h_codes[:].bitcast(FP8X4), scales=h_scales[:], in_=hid)
             for c in range(2):
                 nc.tensor.matmul_mx(
-                    out=sc_ps[h][c], lhsT=h_codes[:].bitcast(FP8X4), lhsT_scale=h_scales[:],
-                    rhs=e_pick[:, spans[c]].bitcast(FP8X4), rhs_scale=es_pick[:, spans[c]], start=True, stop=True,
+                    out=banks[c], lhsT=h_codes[:].bitcast(FP8X4), lhsT_scale=h_scales[:],
+                    rhs=e_pick[:, HALVES[c]].bitcast(FP8X4), rhs_scale=es_pick[:, HALVES[c]], start=True, stop=True,
                 )
 
-        leave_bank(0, 0, False)
-        leave_bank(1, 0, False)
-        leave_bank(0, 1, True)
-        leave_bank(1, 1, False)
-        fetch_delayed(0, 0, True)
-        fetch_delayed(0, 1, True)
-        leave_bank(2, 2, False)
-        leave_bank(3, 2, False)
-        fetch_delayed(1, 0, False)
-        fetch_delayed(1, 1, False)
-        subtract_g(0, 0)
-        subtract_g(0, 1)
-        fetch_delayed(2, 0, True)
-        fetch_delayed(2, 1, True)
-        fetch_delayed(3, 0, False)
-        fetch_delayed(3, 1, False)
-        subtract_g(1, 0)
-        subtract_g(1, 1)
-        join_factors(0)
-        join_factors(1)
-        subtract(2, 2)
-        fetch_es()
-        subtract(3, 2)
-        fetch_e()
-        anchors(0, False)
-        anchors(1, False)
-        anchors_half(2, 0, False)
-        anchors_half(3, 0, False)
-        squash(0)
-        score(0)
-        anchors_half(2, 1, False)
-        anchors_half(3, 1, False)
-        squash(1)
-        score(1)
-
-        off_pick = stage.tile([P, Z], F32, name="off_pick", offset=4608)
-        nc.vector.tensor_copy(off_pick[:], off_tab[:].indirect(fpr_t[:]))
-
+        leave_psum(0, FIRST, nc.scalar.copy)
+        leave_psum(1, FIRST, nc.scalar.copy)
+        leave_psum(0, SECOND, on_vector)
+        leave_psum(1, SECOND, nc.scalar.copy)
+        for span in HALVES:
+            fetch_delayed(0, span, on_vector)
+        for t in range(2, PACK):
+            leave_psum(t, WHOLE, nc.scalar.copy)
+        for span in HALVES:
+            fetch_delayed(1, span, gather_on_scalar)
+        subtract_on_gpsimd(0)
+        for span in HALVES:
+            fetch_delayed(2, span, on_vector)
+        fetch_delayed(3, slice(0, SCALAR_SHARE), gather_on_scalar)
+        fetch_delayed(3, slice(SCALAR_SHARE, S), on_vector)
+        subtract_on_gpsimd(1)
         for h in range(2):
-            squashed = sb.tile([P, Z], F32, name="squashed%d" % h)
-            ks = sb.tile([P, Z], F32, name="ks%d" % h)
-            ko = sb.tile([P, Z], F32, name="ko%d" % h)
-            den = sb.tile([P, 1], F32, name="den%d" % h)
-            inv = sb.tile([P, 1], F32, name="inv%d" % h)
-            mo = sb.tile([P, 1], F32, name="mo%d" % h)
-            for c in ([0, 1] if h == 0 else [2]):
-                nc.scalar.activation(squashed[:, spans[c]], sc_ps[h][c], ACT.Tanh)
-            nc.scalar.activation(ks[:], squashed[:], ACT.Exp, scale=1.4, accum_out=den[:])
-            nc.vector.reciprocal(inv[:], den[:])
-            nc.vector.scalar_tensor_tensor(ko[:], ks[:], inv[:], off_pick[:], ALU.mult, ALU.mult, accum_out=mo[:])
-            for c in ([2] if h == 0 else [0, 1]):
-                res = sb.tile([P, Z], F32, name="res%d%d" % (h, c))
-                nc.vector.scalar_tensor_tensor(res[:, spans[c]], off_pick[:, spans[c]], mo[:], ks[:, spans[c]], ALU.subtract, ALU.mult)
-                queue = nc.scalar if c == 0 else nc.sync
-                queue.dma_start(out=out[h * P : (h + 1) * P, spans[c]], in_=res[:, spans[c]])
+            join_factors(h)
+        subtract_on_vector(2)
+        on_vector(es_pick[:], es_tab[:].indirect(fpr_t[:]))
+        subtract_on_vector(3)
+        on_vector(e_pick[:], e_tab[:].bitcast(U32).indirect(fpr_t[:]))
+
+        for t in range(2):
+            fetch_anchors(t)
+        for t in range(2, PACK):
+            fetch_anchor_half(t, 0)
+        nc.scalar.activation(bits[0][:], picked[:, 0::2, :].rearrange("p t v -> p v t"), ACT.Tanh, scale=2.0)
+        hid0 = shared.tile([P, PACK * P], BF16, name="hid0", offset=AT_E_WORDS, align_bytes=64)
+        sc0 = [ps.tile([P, HALF], F32, name="sc0%d" % c) for c in range(2)]
+        score(0, hid0[:], [bank[:] for bank in sc0])
+
+        off_pick = shared.tile([P, Z], F32, name="off_pick", offset=AT_E_WORDS, align_bytes=64)
+        on_vector(off_pick[:, FIRST], off_tab[:].indirect(entries(fpr_t, FIRST)))
+
+        for t in range(2, PACK):
+            fetch_anchor_half(t, 1)
+        late_rows = picked[:, 1:7, :].rearrange("p (a s) v -> p v a s", s=3)[:, :, :, 0::2]
+        nc.scalar.activation(bits[1][:].rearrange("p v (a b) -> p v a b", b=2), late_rows, ACT.Tanh, scale=2.0)
+        sc1 = ps.tile([P, Z], F32, name="sc1", tag="y_bank2")
+        score(1, off_pick[:, SECOND].bitcast(BF16), [sc1[:, span] for span in HALVES])
+        on_vector(off_pick[:, SECOND], off_tab[:].indirect(entries(fpr_t, SECOND)))
+
+        squashed = [sb.tile([P, Z], F32, name="squashed%d" % h) for h in range(2)]
+        ks = [sb.tile([P, Z], F32, name="ks%d" % h) for h in range(2)]
+        terms = [sb.tile([P, Z], F32, name="terms%d" % h) for h in range(2)]
+        res = [sb.tile([P, Z], F32, name="res%d" % h) for h in range(2)]
+        den = [sb.tile([P, 1], F32, name="den%d" % h) for h in range(2)]
+        inv = [sb.tile([P, 1], F32, name="inv%d" % h) for h in range(2)]
+        mo = [sb.tile([P, 1], F32, name="mo%d" % h) for h in range(2)]
+
+        def exponentiate(h):
+            nc.scalar.activation(ks[h][:], squashed[h][:], ACT.Exp, scale=1.4, accum_out=den[h][:])
+
+        def mean_offset(h):
+            nc.vector.scalar_tensor_tensor(terms[h][:], ks[h][:], inv[h][:], off_pick[:], ALU.mult, ALU.mult, accum_out=mo[h][:])
+
+        def deviate(h, span):
+            nc.vector.scalar_tensor_tensor(res[h][:, span], off_pick[:, span], mo[h][:], ks[h][:, span], ALU.subtract, ALU.mult)
+
+        for c in range(2):
+            nc.scalar.activation(squashed[0][:, HALVES[c]], sc0[c][:], ACT.Tanh)
+        exponentiate(0)
+        nc.scalar.activation(squashed[1][:], sc1[:], ACT.Tanh)
+        exponentiate(1)
+        nc.vector.reciprocal(inv[0][:], den[0][:])
+        mean_offset(0)
+        deviate(0, FIRST)
+        nc.vector.reciprocal(inv[1][:], den[1][:])
+        deviate(0, SECOND)
+        nc.sync.dma_start(out=out[:P, :], in_=res[0][:])
+        mean_offset(1)
+        for span, queue in zip(HALVES, (nc.scalar, nc.sync)):
+            deviate(1, span)
+            queue.dma_start(out=out[P:, span], in_=res[1][:, span])

from contextlib import ExitStack

import concourse.mybir as mybir

K, T, S, H, V, Z, W = 512, 2048, 512, 512, 256, 512, 2048
FLOPS = 2 * K * H * S + 2 * H * V * Z

F32 = mybir.dt.float32
BF16 = mybir.dt.bfloat16
I32 = mybir.dt.int32
U32 = mybir.dt.uint32
U16 = mybir.dt.uint16
U8 = mybir.dt.uint8
FP8X4 = mybir.dt.float8_e4m3fn_x4
ACT = mybir.ActivationFunctionType
ALU = mybir.AluOpType

P = 128
PACK = 4
PER_COLUMN = 16
HALF = 256
FIRST, SECOND, WHOLE = slice(0, HALF), slice(HALF, 2 * HALF), slice(0, 2 * HALF)
HALVES = (FIRST, SECOND)
SCALAR_SHARE = 384

AT_W1 = 0
AT_E_WORDS = 4608
AT_YD = 12800
YD_PITCH = 4096
AT_WEIGHT = AT_YD + YD_PITCH - 1024
AT_E_PICK = AT_YD + 3 * YD_PITCH + 1024
AT_X_WORDS = 29184
AT_E_SCALES = 37376


def tile_picked_yaudfpr_vote_p_kernel(
    tc, x_words, x_scales, w1, rel, e_words, e_scales, unit, off, offs, del_, anc, fpr, out
):
    nc = tc.nc
    with ExitStack() as ctx:
        sb = ctx.enter_context(tc.tile_pool(name="sb", bufs=1))
        shared = ctx.enter_context(tc.tile_pool(name="shared", bufs=1))
        ps = ctx.enter_context(tc.psum_pool(name="ps", bufs=1))

        def entries(list_tile, span):
            return list_tile[:, span.start // PER_COLUMN : span.stop // PER_COLUMN]

        def on_vector(dst, src):
            nc.vector.tensor_copy(dst, src)

        def gather_on_scalar(dst, window):
            nc.scalar.activation(dst, window, ACT.Copy)

        offs_t = sb.tile([P, S // PER_COLUMN], U16, name="offs_t")
        del_t = sb.tile([P, S // PER_COLUMN], U16, name="del_t")
        anc_t = sb.tile([P, V // PER_COLUMN], U16, name="anc_t")
        fpr_t = sb.tile([P, Z // PER_COLUMN], U16, name="fpr_t")
        x_tab = shared.tile([P, T], I32, name="x_tab", offset=AT_X_WORDS)
        xs_tab = sb.tile([P, T], U8, name="xs_tab")
        es_tab = shared.tile([P, W], U8, name="es_tab", offset=AT_E_SCALES)
        w_raw = shared.tile([P, PACK, H], F32, name="w_raw", offset=AT_W1)

        def load_words(tab, words):
            nc.sync.dma_start(out=tab[:], in_=words[0].rearrange("p n j -> p (n j)").bitcast(I32))

        def load_scales(tab, scales):
            for q in range(4):
                rows = scales[0, 4 * q : 4 * q + 4, :]
                nc.sync.dma_start(out=tab[32 * q : 32 * q + 4, :].bitcast(I32), in_=rows.bitcast(I32))

        nc.gpsimd.memset(xs_tab[:, : T // 2].bitcast(I32), 0)
        nc.vector.memset(xs_tab[:, T // 2 :].bitcast(I32), 0)
        nc.vector.memset(es_tab[:].bitcast(I32), 0)
        nc.sync.dma_start(offs_t[:], offs)
        nc.sync.dma_start(fpr_t[:], fpr)
        nc.sync.dma_start(out=w_raw[:], in_=w1.rearrange("(p j) c -> p j c", j=PACK))
        load_scales(xs_tab, x_scales)
        nc.sync.dma_start(del_t[:], del_)
        nc.sync.dma_start(anc_t[:], anc)
        load_words(x_tab, x_words)
        load_scales(es_tab, e_scales)

        xs_pick = sb.tile([P, S], U8, name="xs_pick", align_bytes=64)
        x_pick = [sb.tile([P, HALF], U32, name="x_pick%d" % c, align_bytes=64) for c in range(2)]
        es_pick = sb.tile([P, Z], U8, name="es_pick", align_bytes=64)
        on_vector(xs_pick[:], xs_tab[:].indirect(offs_t[:]))

        w_bf = [sb.tile([P, 2, P, PACK], BF16, name="w_bf%d" % u, tag="w_bf%d" % u, align_bytes=64) for u in range(2)]
        w_cols = w_raw[:].rearrange("p j (m t) -> p m j t", t=PACK)
        for u in range(2):
            nc.scalar.copy(w_bf[u][:].rearrange("p s m j -> p m j s"), w_cols[:, :, :, 2 * u : 2 * u + 2])

        w_codes = [sb.tile([P, P], U32, name="w_codes%d" % t, align_bytes=64) for t in range(2)]
        for t in range(2, PACK):
            w_codes.append(shared.tile([P, P], U32, name="w_codes%d" % t, offset=AT_X_WORDS + 4 * P * t, align_bytes=64))
        w_scales = [sb.tile([P, P], U8, name="w_scales%d" % t, align_bytes=64) for t in range(PACK)]

        def quantize_w(t):
            values = w_bf[t // 2][:, t % 2].rearrange("p m j -> p (m j)")
            nc.vector.quantize_mx(out=w_codes[t][:].bitcast(FP8X4), scales=w_scales[t][:], in_=values)

        quantize_w(0)
        quantize_w(1)
        for c in range(2):
            on_vector(x_pick[c][:], x_tab[:].bitcast(U32).indirect(entries(offs_t, HALVES[c])))
        quantize_w(2)
        quantize_w(3)

        factors = shared.tile([P, PACK * V + PACK], F32, name="factors", offset=AT_W1)
        e_tab = shared.tile([P, W], I32, name="e_tab", offset=AT_E_WORDS)
        off_tab = sb.tile([P, W], F32, name="off_tab", tag="w_bf1", align_bytes=64)
        nc.sync.dma_start(out=factors[:, : PACK * V], in_=rel.rearrange("(p t) v -> p (t v)", t=PACK))
        nc.sync.dma_start(out=factors[:, PACK * V :], in_=unit.rearrange("(p t) o -> p (t o)", t=PACK))
        load_words(e_tab, e_words)
        nc.sync.dma_start(out=off_tab[:], in_=off)

        y_ps = {}
        for t in range(2):
            for c in range(2):
                y_ps[t, HALVES[c].start] = ps.tile([P, HALF], F32, name="y_ps%d%d" % (t, c))
        y_bank = {t: ps.tile([P, S], F32, name="y_bank%d" % t, tag="y_bank%d" % t) for t in range(2, PACK)}

        def y_in_psum(t, span):
            return y_ps[t, span.start][:] if t < 2 else y_bank[t][:, span]

        y_sb = [sb.tile([P, S], F32, name="y_sb%d" % t) for t in range(PACK)]
        for t in range(PACK):
            for c in range(2):
                nc.tensor.matmul_mx(
                    out=y_in_psum(t, HALVES[c]), lhsT=w_codes[t][:].bitcast(FP8X4), lhsT_scale=w_scales[t][:],
                    rhs=x_pick[c][:].bitcast(FP8X4), rhs_scale=xs_pick[:, HALVES[c]], start=True, stop=True,
                )

        yd = [shared.tile([P, S], F32, name="yd%d" % t, offset=AT_YD + YD_PITCH * t) for t in range(PACK)]
        dif = [sb.tile([P, S], F32, name="dif%d" % t) for t in range(PACK - 1)]
        dif.append(shared.tile([P, S], F32, name="dif3", offset=AT_E_SCALES))
        picked = sb.tile([P, 7, P], F32, name="picked")
        bits = [sb.tile([P, P, PACK], F32, name="bits%d" % h) for h in range(2)]
        weight = [shared.tile([P, P, PACK], F32, name="weight%d" % h, offset=AT_WEIGHT + 4 * P * PACK * h) for h in range(2)]
        e_pick = shared.tile([P, Z], U32, name="e_pick", offset=AT_E_PICK, align_bytes=64)

        def leave_psum(t, span, copy):
            copy(y_sb[t][:, span], y_in_psum(t, span))

        def fetch_delayed(t, span, gather):
            gather(yd[t][:, span], y_sb[t][:].indirect(entries(del_t, span)))

        def subtract_on_gpsimd(t):
            for span in HALVES:
                nc.gpsimd.tensor_tensor(dif[t][:, span], y_sb[t][:, span], yd[t][:, span], ALU.subtract)

        def subtract_on_vector(t):
            nc.vector.tensor_tensor(dif[t][:], y_in_psum(t, WHOLE), yd[t][:], ALU.subtract)

        def fetch_anchors(t):
            gather_on_scalar(picked[:, 2 * t : 2 * t + 2, :].rearrange("p h v -> p (h v)"), dif[t][:].indirect(anc_t[:]))

        def fetch_anchor_half(t, h):
            gather_on_scalar(picked[:, 2 * t, :], dif[t][:].indirect(entries(anc_t, slice(h * P, (h + 1) * P))))

        def join_factors(h):
            rel_h = factors[:, : PACK * V].rearrange("p (t v) -> p v t", t=PACK)[:, h * P : (h + 1) * P, :]
            unit_b = factors[:, PACK * V :].unsqueeze(1).to_broadcast([P, P, PACK])
            nc.gpsimd.tensor_tensor(weight[h][:], rel_h, unit_b, ALU.mult)

        def score(h, hid, banks):
            nc.vector.tensor_tensor(hid, bits[h][:].rearrange("p v t -> p (v t)"), weight[h][:].rearrange("p v t -> p (v t)"), ALU.mult)
            h_codes = sb.tile([P, P], U32, name="h_codes%d" % h, align_bytes=64)
            h_scales = sb.tile([P, P], U8, name="h_scales%d" % h, align_bytes=64)
            nc.vector.quantize_mx(out=h_codes[:].bitcast(FP8X4), scales=h_scales[:], in_=hid)
            for c in range(2):
                nc.tensor.matmul_mx(
                    out=banks[c], lhsT=h_codes[:].bitcast(FP8X4), lhsT_scale=h_scales[:],
                    rhs=e_pick[:, HALVES[c]].bitcast(FP8X4), rhs_scale=es_pick[:, HALVES[c]], start=True, stop=True,
                )

        leave_psum(0, FIRST, nc.scalar.copy)
        leave_psum(1, FIRST, nc.scalar.copy)
        leave_psum(0, SECOND, on_vector)
        leave_psum(1, SECOND, nc.scalar.copy)
        for span in HALVES:
            fetch_delayed(0, span, on_vector)
        for t in range(2, PACK):
            leave_psum(t, WHOLE, nc.scalar.copy)
        for span in HALVES:
            fetch_delayed(1, span, gather_on_scalar)
        subtract_on_gpsimd(0)
        for span in HALVES:
            fetch_delayed(2, span, on_vector)
        fetch_delayed(3, slice(0, SCALAR_SHARE), gather_on_scalar)
        fetch_delayed(3, slice(SCALAR_SHARE, S), on_vector)
        subtract_on_gpsimd(1)
        for h in range(2):
            join_factors(h)
        subtract_on_vector(2)
        on_vector(es_pick[:], es_tab[:].indirect(fpr_t[:]))
        subtract_on_vector(3)
        on_vector(e_pick[:], e_tab[:].bitcast(U32).indirect(fpr_t[:]))

        for t in range(2):
            fetch_anchors(t)
        for t in range(2, PACK):
            fetch_anchor_half(t, 0)
        nc.scalar.activation(bits[0][:], picked[:, 0::2, :].rearrange("p t v -> p v t"), ACT.Tanh, scale=2.0)
        hid0 = shared.tile([P, PACK * P], BF16, name="hid0", offset=AT_E_WORDS, align_bytes=64)
        sc0 = [ps.tile([P, HALF], F32, name="sc0%d" % c) for c in range(2)]
        score(0, hid0[:], [bank[:] for bank in sc0])

        off_pick = shared.tile([P, Z], F32, name="off_pick", offset=AT_E_WORDS, align_bytes=64)
        on_vector(off_pick[:, FIRST], off_tab[:].indirect(entries(fpr_t, FIRST)))

        for t in range(2, PACK):
            fetch_anchor_half(t, 1)
        late_rows = picked[:, 1:7, :].rearrange("p (a s) v -> p v a s", s=3)[:, :, :, 0::2]
        nc.scalar.activation(bits[1][:].rearrange("p v (a b) -> p v a b", b=2), late_rows, ACT.Tanh, scale=2.0)
        sc1 = ps.tile([P, Z], F32, name="sc1", tag="y_bank2")
        score(1, off_pick[:, SECOND].bitcast(BF16), [sc1[:, span] for span in HALVES])
        on_vector(off_pick[:, SECOND], off_tab[:].indirect(entries(fpr_t, SECOND)))

        squashed = [sb.tile([P, Z], F32, name="squashed%d" % h) for h in range(2)]
        ks = [sb.tile([P, Z], F32, name="ks%d" % h) for h in range(2)]
        terms = [sb.tile([P, Z], F32, name="terms%d" % h) for h in range(2)]
        res = [sb.tile([P, Z], F32, name="res%d" % h) for h in range(2)]
        den = [sb.tile([P, 1], F32, name="den%d" % h) for h in range(2)]
        inv = [sb.tile([P, 1], F32, name="inv%d" % h) for h in range(2)]
        mo = [sb.tile([P, 1], F32, name="mo%d" % h) for h in range(2)]

        def exponentiate(h):
            nc.scalar.activation(ks[h][:], squashed[h][:], ACT.Exp, scale=1.4, accum_out=den[h][:])

        def mean_offset(h):
            nc.vector.scalar_tensor_tensor(terms[h][:], ks[h][:], inv[h][:], off_pick[:], ALU.mult, ALU.mult, accum_out=mo[h][:])

        def deviate(h, span):
            nc.vector.scalar_tensor_tensor(res[h][:, span], off_pick[:, span], mo[h][:], ks[h][:, span], ALU.subtract, ALU.mult)

        for c in range(2):
            nc.scalar.activation(squashed[0][:, HALVES[c]], sc0[c][:], ACT.Tanh)
        exponentiate(0)
        nc.scalar.activation(squashed[1][:], sc1[:], ACT.Tanh)
        exponentiate(1)
        nc.vector.reciprocal(inv[0][:], den[0][:])
        mean_offset(0)
        deviate(0, FIRST)
        nc.vector.reciprocal(inv[1][:], den[1][:])
        deviate(0, SECOND)
        nc.sync.dma_start(out=out[:P, :], in_=res[0][:])
        mean_offset(1)
        for span, queue in zip(HALVES, (nc.scalar, nc.sync)):
            deviate(1, span)
            queue.dma_start(out=out[P:, span], in_=res[1][:, span])
